import numpy as np
import ml_dtypes


def mxq(x, axis, fmt="e4m3"):
    dtype, down = {"e4m3": (ml_dtypes.float8_e4m3fn, 7), "e5m2": (ml_dtypes.float8_e5m2, 14)}[fmt]
    v = np.moveaxis(np.asarray(x, np.float32).astype(ml_dtypes.bfloat16).astype(np.float64), axis, -1)
    blocks = v.reshape(v.shape[:-1] + (-1, 32))
    amax = np.abs(blocks).max(-1, keepdims=True)
    byte = np.maximum(np.where(amax > 0, np.frexp(amax)[1] - 1 + 127, 0) - down, 1)
    scale = np.exp2(byte - 127.0)
    codes = (blocks / scale).astype(np.float32).astype(dtype).astype(np.float64)
    return np.moveaxis((codes * scale).reshape(v.shape), -1, axis)


WIDE = False


def mx_kscale(k):
    if not WIDE:
        return np.ones(k)
    levels = np.array([10, -10, 5, -5, 0])
    if k % 512:
        return np.exp2(np.random.permutation(np.resize(levels, k // 32))).repeat(32)
    a = np.empty((k // 512, 16))
    for p in range(k // 512):
        a[p, :8] = np.random.permutation(np.resize(levels, 8))
        for g in range(8):
            far = levels[np.abs(levels - a[p, g]) >= 10]
            a[p, g + 8] = far[np.random.randint(len(far))]
    return np.exp2(a.ravel()).repeat(32)


def f64(x):
    return np.asarray(x).astype(np.float64)


def striped8(idx):
    return np.concatenate([v.reshape(-1, 16).T for v in idx]).astype(np.uint16)


def unstriped8(offs):
    return np.stack([offs[16 * g:16 * g + 16].T.reshape(-1) for g in range(8)]).astype(np.int64)


K, M, T, S = 512, 1024, 4096, 2048


def setup_inputs():
    n = np.random.standard_normal
    s = mx_kscale(K)[:, None]
    return {
        "x": (n((K, S)) * s).astype(np.float32),
        "w": (n((K, M)) / np.sqrt(K) / s).astype(np.float32),
        "wgo": np.repeat(np.random.uniform(0.5, 2.0, (8, S)), 16, axis=0).astype(np.float32),
        "offs": striped8(np.stack([np.random.permutation(T)[:S] for _ in range(8)])),
    }


def reference(x, w, wgo, offs):
    x_ = mxq(f64(x), 0, "e4m3")
    w_ = mxq(f64(w), 0, "e4m3")
    y = w_.T @ x_
    place = unstriped8(offs)[np.arange(M) % 128 // 16]
    out = np.zeros((M, T))
    out[np.arange(M)[:, None], place] = f64(wgo)[np.arange(M) % 128] * (y)
    return out

@@ -1,0 +1,168 @@
+from contextlib import ExitStack
+
+import concourse.mybir as mybir
+
+K, M, T, S = 512, 1024, 4096, 2048
+FLOPS = 2 * K * M * S
+
+F32 = mybir.dt.float32
+BF16 = mybir.dt.bfloat16
+U32 = mybir.dt.uint32
+U16 = mybir.dt.uint16
+U8 = mybir.dt.uint8
+FP8X4 = mybir.dt.float8_e4m3fn_x4
+MULT = mybir.AluOpType.mult
+
+P = 128
+PACK = 4
+HALF = S // 2
+BANK = 512
+
+
+def tile_list_hscat_none_kernel(tc, x, w, wgo, offs, out):
+    nc = tc.nc
+    with ExitStack() as ctx:
+        lists = ctx.enter_context(tc.tile_pool(name="lists", bufs=1))
+        keep = ctx.enter_context(tc.tile_pool(name="keep", bufs=1))
+        ring = ctx.enter_context(tc.tile_pool(name="ring", bufs=6))
+        psum = ctx.enter_context(tc.psum_pool(name="psum", bufs=8))
+
+        offsets = lists.tile([P, S // 16], U16, name="offsets")
+
+        def load(src, c0, width, name):
+            raw = keep.tile([P, PACK, width], F32, name="raw_" + name)
+            nc.sync.dma_start(out=raw[:], in_=src[:, c0 : c0 + width].rearrange("(p j) c -> p j c", j=PACK))
+            return raw
+
+        def operand(width, name, tag=None):
+            grouped = keep.tile([P, width, PACK], BF16, align_bytes=64, tag=tag or "grouped_" + name, name="grouped_" + name)
+            codes = keep.tile([P, width], U32, align_bytes=64, name="codes_" + name)
+            scales = keep.tile([P, width], U8, align_bytes=64, name="scales_" + name)
+            return grouped, codes, scales
+
+        def interleave(copy, grouped, raw, g0, r0, width):
+            copy(
+                out=grouped[:, g0 : g0 + width, :].rearrange("p (c i) j -> p c j i", i=4),
+                in_=raw[:, :, r0 : r0 + width].rearrange("p j (c i) -> p c j i", i=4),
+            )
+
+        def quantise(op):
+            grouped, codes, scales = op
+            nc.vector.quantize_mx(
+                out=codes[:].bitcast(FP8X4), scales=scales[:], in_=grouped[:].rearrange("p c j -> p (c j)")
+            )
+
+        def multiply(w_op, w0, x_op, width):
+            acc = psum.tile([P, BANK], F32, name="acc")
+            nc.tensor.matmul_mx(
+                out=acc[:, :width],
+                lhsT=w_op[1][:, w0 : w0 + P].bitcast(FP8X4),
+                lhsT_scale=w_op[2][:, w0 : w0 + P],
+                rhs=x_op[1][:].bitcast(FP8X4),
+                rhs_scale=x_op[2][:],
+                start=True,
+                stop=True,
+            )
+            return acc
+
+        vcopy, scopy = nc.vector.tensor_copy, nc.scalar.copy
+
+        raw_w = {}
+        raw_w[0] = load(w, 0, 128, "w0")
+        raw_xa = load(x, 0, 512, "xa")
+        raw_xb = load(x, 512, 256, "xb")
+        raw_xc = load(x, 768, 256, "xc")
+        raw_w[1] = load(w, 128, 128, "w1")
+        nc.sync.dma_start(offsets[:], offs)
+        wgo_half = [keep.tile([P, HALF], F32, name="wgo0"), keep.tile([P, HALF], F32, name="wgo1")]
+        nc.sync.dma_start(out=wgo_half[0][:], in_=wgo[:, 0:HALF])
+        raw_w[2] = load(w, 256, 256, "w2")
+        raw_xd = load(x, 1024, 512, "xd")
+        raw_xe = load(x, 1536, 512, "xe")
+        raw_w[4] = load(w, 512, 512, "w4")
+        nc.sync.dma_start(out=wgo_half[1][:], in_=wgo[:, HALF:S])
+
+        windows = []
+
+        def window(tag):
+            tile = keep.tile([P, T], F32, align_bytes=64, tag=tag, name="window")
+            nc.gpsimd.memset(tile[:], 0.0)
+            windows.append(tile)
+
+        window("window0")
+
+        w_ops = {}
+        w_ops[0] = operand(128, "w0")
+        interleave(scopy, w_ops[0][0], raw_w[0], 0, 0, 128)
+        quantise(w_ops[0])
+        x0 = [operand(256, "x0"), operand(256, "x1"), operand(256, "x2"), operand(256, "x3")]
+        interleave(scopy, x0[0][0], raw_xa, 0, 0, 256)
+        interleave(vcopy, x0[1][0], raw_xa, 0, 256, 256)
+        quantise(x0[0])
+        quantise(x0[1])
+        interleave(vcopy, x0[2][0], raw_xb, 0, 0, 256)
+        quantise(x0[2])
+        interleave(scopy, x0[3][0], raw_xc, 160, 160, 96)
+        interleave(vcopy, x0[3][0], raw_xc, 0, 0, 160)
+        quantise(x0[3])
+        w_ops[1] = operand(128, "w1", "slot1")
+        interleave(scopy, w_ops[1][0], raw_w[1], 0, 0, 128)
+
+        def weights(m):
+            if m < 2:
+                return w_ops[m], 0
+            if m < 4:
+                return w_ops[2], (m - 2) * P
+            return w_ops[4], (m - 4) * P
+
+        def project(m, h):
+            y = ring.tile([P, HALF], F32, name="y")
+            w_op, w0 = weights(m)
+            if h == 0:
+                for q in range(4):
+                    acc = multiply(w_op, w0, x0[q], 256)
+                    copy = vcopy if m == 0 and q in (0, 2) else scopy
+                    copy(out=y[:, q * 256 : (q + 1) * 256], in_=acc[:, :256])
+            else:
+                for q in range(2):
+                    acc = multiply(w_op, w0, x1[q], 512)
+                    scopy(out=y[:, q * 512 : (q + 1) * 512], in_=acc[:])
+            return y
+
+        def scatter(m, h, y):
+            nc.vector.tensor_tensor(
+                windows[m % 3][:].indirect(offsets[:, h * 64 : (h + 1) * 64]), y[:], wgo_half[h][:], MULT
+            )
+            if h == 1:
+                nc.sync.dma_start(out=out[m * P : (m + 1) * P, :], in_=windows[m % 3][:])
+
+        steps = [(0, 0), (1, 0), (2, 0), (0, 1), (1, 1), (3, 0), (2, 1), (4, 0), (3, 1), (5, 0), (4, 1), (6, 0), (5, 1), (7, 0), (6, 1), (7, 1)]
+        y = project(0, 0)
+        quantise(w_ops[1])
+        window("slot1")
+        y_next = project(1, 0)
+        scatter(0, 0, y)
+
+        w_ops[2] = operand(256, "w2", "slot2")
+        interleave(scopy, w_ops[2][0], raw_w[2], 0, 0, 256)
+        quantise(w_ops[2])
+        window("slot2")
+        y, y_next = y_next, project(2, 0)
+        scatter(1, 0, y)
+
+        x1 = [operand(512, "x4"), operand(512, "x5")]
+        interleave(scopy, x1[0][0], raw_xd, 0, 0, 512)
+        quantise(x1[0])
+        interleave(scopy, x1[1][0], raw_xe, 0, 0, 512)
+        quantise(x1[1])
+        y, y_next = y_next, project(0, 1)
+        scatter(2, 0, y)
+
+        w_ops[4] = operand(512, "w4")
+        interleave(scopy, w_ops[4][0], raw_w[4], 0, 0, 512)
+        quantise(w_ops[4])
+        for i in range(3, len(steps)):
+            y = y_next
+            if i + 1 < len(steps):
+                y_next = project(*steps[i + 1])
+            scatter(*steps[i], y)

@@ -136,7 +136,7 @@ def tile_list_hscat_none_kernel(tc, x, w, wgo, offs, out):
             if h == 1:
                 nc.sync.dma_start(out=out[m * P : (m + 1) * P, :], in_=windows[m % 3][:])
 
-        steps = [(0, 0), (1, 0), (2, 0), (0, 1), (1, 1), (3, 0), (2, 1), (4, 0), (3, 1), (5, 0), (4, 1), (6, 0), (5, 1), (7, 0), (6, 1), (7, 1)]
+        steps = [(m, h) for first in (0, 3, 6) for h in range(2) for m in range(first, min(first + 3, M // P))]
         y = project(0, 0)
         quantise(w_ops[1])
         window("slot1")

@@ -16,7 +16,12 @@ MULT = mybir.AluOpType.mult
 P = 128
 PACK = 4
 HALF = S // 2
+HALF_OFFSETS = HALF // 16
+PIECE = 256
 BANK = 512
+WINDOWS = 4
+Y_BUFS = 6
+VECTOR_SHARE = 160
 
 
 def tile_list_hscat_none_kernel(tc, x, w, wgo, offs, out):
@@ -24,40 +29,42 @@ def tile_list_hscat_none_kernel(tc, x, w, wgo, offs, out):
     with ExitStack() as ctx:
         lists = ctx.enter_context(tc.tile_pool(name="lists", bufs=1))
         keep = ctx.enter_context(tc.tile_pool(name="keep", bufs=1))
-        ring = ctx.enter_context(tc.tile_pool(name="ring", bufs=6))
+        products = ctx.enter_context(tc.tile_pool(name="products", bufs=Y_BUFS))
         psum = ctx.enter_context(tc.psum_pool(name="psum", bufs=8))
 
-        offsets = lists.tile([P, S // 16], U16, name="offsets")
-
-        def load(src, c0, width, name):
-            raw = keep.tile([P, PACK, width], F32, name="raw_" + name)
-            nc.sync.dma_start(out=raw[:], in_=src[:, c0 : c0 + width].rearrange("(p j) c -> p j c", j=PACK))
+        def load(src, first, width, name, tag=None):
+            raw = keep.tile([P, PACK, width], F32, align_bytes=64, tag=tag or "raw_" + name, name="raw_" + name)
+            nc.sync.dma_start(
+                out=raw[:], in_=src[:, first : first + width].rearrange("(p i) c -> p i c", i=PACK)
+            )
             return raw
 
         def operand(width, name, tag=None):
-            grouped = keep.tile([P, width, PACK], BF16, align_bytes=64, tag=tag or "grouped_" + name, name="grouped_" + name)
+            grouped = keep.tile(
+                [P, width, PACK], BF16, align_bytes=64, tag=tag or "grouped_" + name, name="grouped_" + name
+            )
             codes = keep.tile([P, width], U32, align_bytes=64, name="codes_" + name)
             scales = keep.tile([P, width], U8, align_bytes=64, name="scales_" + name)
             return grouped, codes, scales
 
-        def interleave(copy, grouped, raw, g0, r0, width):
+        def interleave(copy, op, raw, to, first, width):
             copy(
-                out=grouped[:, g0 : g0 + width, :].rearrange("p (c i) j -> p c j i", i=4),
-                in_=raw[:, :, r0 : r0 + width].rearrange("p j (c i) -> p c j i", i=4),
+                out=op[0][:, to : to + width, :].rearrange("p (c b) i -> p c i b", b=4),
+                in_=raw[:, :, first : first + width].rearrange("p i (c b) -> p c i b", b=4),
             )
 
         def quantise(op):
             grouped, codes, scales = op
             nc.vector.quantize_mx(
-                out=codes[:].bitcast(FP8X4), scales=scales[:], in_=grouped[:].rearrange("p c j -> p (c j)")
+                out=codes[:].bitcast(FP8X4), scales=scales[:], in_=grouped[:].rearrange("p c i -> p (c i)")
             )
 
-        def multiply(w_op, w0, x_op, width):
+        def multiply(weights, first, x_op, width):
             acc = psum.tile([P, BANK], F32, name="acc")
             nc.tensor.matmul_mx(
                 out=acc[:, :width],
-                lhsT=w_op[1][:, w0 : w0 + P].bitcast(FP8X4),
-                lhsT_scale=w_op[2][:, w0 : w0 + P],
+                lhsT=weights[1][:, first : first + P].bitcast(FP8X4),
+                lhsT_scale=weights[2][:, first : first + P],
                 rhs=x_op[1][:].bitcast(FP8X4),
                 rhs_scale=x_op[2][:],
                 start=True,
@@ -65,102 +72,95 @@ def tile_list_hscat_none_kernel(tc, x, w, wgo, offs, out):
             )
             return acc
 
-        vcopy, scopy = nc.vector.tensor_copy, nc.scalar.copy
+        by_vector, by_scalar = nc.vector.tensor_copy, nc.scalar.copy
 
-        raw_w = {}
-        raw_w[0] = load(w, 0, 128, "w0")
-        raw_xa = load(x, 0, 512, "xa")
-        raw_xb = load(x, 512, 256, "xb")
-        raw_xc = load(x, 768, 256, "xc")
-        raw_w[1] = load(w, 128, 128, "w1")
+        raw_w0 = load(w, 0, P, "w0")
+        raw_xa = load(x, 0, 2 * PIECE, "xa")
+        raw_xb = load(x, 2 * PIECE, PIECE, "xb")
+        raw_xc = load(x, 3 * PIECE, PIECE, "xc")
+        raw_w1 = load(w, P, P, "w1")
+        offsets = lists.tile([P, S // 16], U16, name="offsets")
         nc.sync.dma_start(offsets[:], offs)
-        wgo_half = [keep.tile([P, HALF], F32, name="wgo0"), keep.tile([P, HALF], F32, name="wgo1")]
-        nc.sync.dma_start(out=wgo_half[0][:], in_=wgo[:, 0:HALF])
-        raw_w[2] = load(w, 256, 256, "w2")
-        raw_xd = load(x, 1024, 512, "xd")
-        raw_xe = load(x, 1536, 512, "xe")
-        raw_w[4] = load(w, 512, 512, "w4")
-        nc.sync.dma_start(out=wgo_half[1][:], in_=wgo[:, HALF:S])
+        wgo_halves = [keep.tile([P, HALF], F32, name="wgo0"), keep.tile([P, HALF], F32, name="wgo1")]
+        nc.sync.dma_start(out=wgo_halves[0][:], in_=wgo[:, :HALF])
+        raw_w2 = load(w, 2 * P, 2 * P, "w2")
+        raw_xd = load(x, HALF, BANK, "xd", tag="bytes3")
+        raw_xe = load(x, HALF + BANK, BANK, "xe")
+        raw_w4 = load(w, 4 * P, 4 * P, "w4")
+        nc.sync.dma_start(out=wgo_halves[1][:], in_=wgo[:, HALF:])
 
         windows = []
 
-        def window(tag):
-            tile = keep.tile([P, T], F32, align_bytes=64, tag=tag, name="window")
-            nc.gpsimd.memset(tile[:], 0.0)
-            windows.append(tile)
+        def add_window(tag):
+            window = keep.tile([P, T], F32, align_bytes=64, tag=tag, name="window")
+            nc.gpsimd.memset(window[:], 0.0)
+            windows.append(window)
 
-        window("window0")
+        add_window("bytes0")
 
-        w_ops = {}
-        w_ops[0] = operand(128, "w0")
-        interleave(scopy, w_ops[0][0], raw_w[0], 0, 0, 128)
-        quantise(w_ops[0])
-        x0 = [operand(256, "x0"), operand(256, "x1"), operand(256, "x2"), operand(256, "x3")]
-        interleave(scopy, x0[0][0], raw_xa, 0, 0, 256)
-        interleave(vcopy, x0[1][0], raw_xa, 0, 256, 256)
-        quantise(x0[0])
-        quantise(x0[1])
-        interleave(vcopy, x0[2][0], raw_xb, 0, 0, 256)
-        quantise(x0[2])
-        interleave(scopy, x0[3][0], raw_xc, 160, 160, 96)
-        interleave(vcopy, x0[3][0], raw_xc, 0, 0, 160)
-        quantise(x0[3])
-        w_ops[1] = operand(128, "w1", "slot1")
-        interleave(scopy, w_ops[1][0], raw_w[1], 0, 0, 128)
+        w0 = operand(P, "w0")
+        interleave(by_scalar, w0, raw_w0, 0, 0, P)
+        quantise(w0)
+        x_first = [operand(PIECE, "x0"), operand(PIECE, "x1"), operand(PIECE, "x2"), operand(PIECE, "x3")]
+        interleave(by_scalar, x_first[0], raw_xa, 0, 0, PIECE)
+        interleave(by_vector, x_first[1], raw_xa, 0, PIECE, PIECE)
+        quantise(x_first[0])
+        quantise(x_first[1])
+        interleave(by_vector, x_first[2], raw_xb, 0, 0, PIECE)
+        quantise(x_first[2])
+        interleave(by_scalar, x_first[3], raw_xc, VECTOR_SHARE, VECTOR_SHARE, PIECE - VECTOR_SHARE)
+        interleave(by_vector, x_first[3], raw_xc, 0, 0, VECTOR_SHARE)
+        quantise(x_first[3])
 
-        def weights(m):
-            if m < 2:
-                return w_ops[m], 0
-            if m < 4:
-                return w_ops[2], (m - 2) * P
-            return w_ops[4], (m - 4) * P
+        w1 = operand(P, "w1", tag="bytes1")
+        w2 = operand(2 * P, "w2", tag="bytes2")
+        w4 = operand(4 * P, "w4")
+        x_second = [operand(BANK, "x4"), operand(BANK, "x5")]
+        interleave(by_scalar, w1, raw_w1, 0, 0, P)
+
+        weights_of = [(w0, 0), (w1, 0), (w2, 0), (w2, P)] + [(w4, m * P) for m in range(4)]
 
         def project(m, h):
-            y = ring.tile([P, HALF], F32, name="y")
-            w_op, w0 = weights(m)
-            if h == 0:
-                for q in range(4):
-                    acc = multiply(w_op, w0, x0[q], 256)
-                    copy = vcopy if m == 0 and q in (0, 2) else scopy
-                    copy(out=y[:, q * 256 : (q + 1) * 256], in_=acc[:, :256])
-            else:
-                for q in range(2):
-                    acc = multiply(w_op, w0, x1[q], 512)
-                    scopy(out=y[:, q * 512 : (q + 1) * 512], in_=acc[:])
+            y = products.tile([P, HALF], F32, name="y")
+            weights, first = weights_of[m]
+            pieces, width = (x_first, PIECE) if h == 0 else (x_second, BANK)
+            for q, piece in enumerate(pieces):
+                acc = multiply(weights, first, piece, width)
+                copy = by_vector if (m, h) == (0, 0) and q % 2 == 0 else by_scalar
+                copy(out=y[:, q * width : (q + 1) * width], in_=acc[:, :width])
             return y
 
+        steps = [(m, h) for group in (0, WINDOWS) for h in range(2) for m in range(group, group + WINDOWS)]
+
         def scatter(m, h, y):
-            nc.vector.tensor_tensor(
-                windows[m % 3][:].indirect(offsets[:, h * 64 : (h + 1) * 64]), y[:], wgo_half[h][:], MULT
-            )
+            window = windows[m % WINDOWS]
+            places = offsets[:, h * HALF_OFFSETS : (h + 1) * HALF_OFFSETS]
+            nc.vector.tensor_tensor(window[:].indirect(places), y[:], wgo_halves[h][:], MULT)
             if h == 1:
-                nc.sync.dma_start(out=out[m * P : (m + 1) * P, :], in_=windows[m % 3][:])
+                nc.sync.dma_start(out=out[m * P : (m + 1) * P, :], in_=window[:])
 
-        steps = [(m, h) for first in (0, 3, 6) for h in range(2) for m in range(first, min(first + 3, M // P))]
-        y = project(0, 0)
-        quantise(w_ops[1])
-        window("slot1")
-        y_next = project(1, 0)
-        scatter(0, 0, y)
+        y = project(*steps[0])
+        quantise(w1)
+        add_window("bytes1")
+        y_next = project(*steps[1])
+        scatter(*steps[0], y)
 
-        w_ops[2] = operand(256, "w2", "slot2")
-        interleave(scopy, w_ops[2][0], raw_w[2], 0, 0, 256)
-        quantise(w_ops[2])
-        window("slot2")
-        y, y_next = y_next, project(2, 0)
-        scatter(1, 0, y)
+        interleave(by_scalar, w2, raw_w2, 0, 0, 2 * P)
+        quantise(w2)
+        add_window("bytes2")
+        interleave(by_scalar, x_second[0], raw_xd, 0, 0, BANK)
+        add_window("bytes3")
+        interleave(by_scalar, x_second[1], raw_xe, 0, 0, BANK)
+        y, y_next = y_next, project(*steps[2])
+        scatter(*steps[1], y)
 
-        x1 = [operand(512, "x4"), operand(512, "x5")]
-        interleave(scopy, x1[0][0], raw_xd, 0, 0, 512)
-        quantise(x1[0])
-        interleave(scopy, x1[1][0], raw_xe, 0, 0, 512)
-        quantise(x1[1])
-        y, y_next = y_next, project(0, 1)
-        scatter(2, 0, y)
+        y, y_next = y_next, project(*steps[3])
+        scatter(*steps[2], y)
 
-        w_ops[4] = operand(512, "w4")
-        interleave(scopy, w_ops[4][0], raw_w[4], 0, 0, 512)
-        quantise(w_ops[4])
+        quantise(x_second[0])
+        quantise(x_second[1])
+        interleave(by_scalar, w4, raw_w4, 0, 0, 4 * P)
+        quantise(w4)
         for i in range(3, len(steps)):
             y = y_next
             if i + 1 < len(steps):

@@ -32,8 +32,8 @@ def tile_list_hscat_none_kernel(tc, x, w, wgo, offs, out):
         products = ctx.enter_context(tc.tile_pool(name="products", bufs=Y_BUFS))
         psum = ctx.enter_context(tc.psum_pool(name="psum", bufs=8))
 
-        def load(src, first, width, name, tag=None):
-            raw = keep.tile([P, PACK, width], F32, align_bytes=64, tag=tag or "raw_" + name, name="raw_" + name)
+        def load(src, first, width, name):
+            raw = keep.tile([P, PACK, width], F32, name="raw_" + name)
             nc.sync.dma_start(
                 out=raw[:], in_=src[:, first : first + width].rearrange("(p i) c -> p i c", i=PACK)
             )
@@ -84,19 +84,19 @@ def tile_list_hscat_none_kernel(tc, x, w, wgo, offs, out):
         wgo_halves = [keep.tile([P, HALF], F32, name="wgo0"), keep.tile([P, HALF], F32, name="wgo1")]
         nc.sync.dma_start(out=wgo_halves[0][:], in_=wgo[:, :HALF])
         raw_w2 = load(w, 2 * P, 2 * P, "w2")
-        raw_xd = load(x, HALF, BANK, "xd", tag="bytes3")
+        raw_xd = load(x, HALF, BANK, "xd")
         raw_xe = load(x, HALF + BANK, BANK, "xe")
         raw_w4 = load(w, 4 * P, 4 * P, "w4")
         nc.sync.dma_start(out=wgo_halves[1][:], in_=wgo[:, HALF:])
 
         windows = []
 
-        def add_window(tag):
+        def add_window(engine, tag):
             window = keep.tile([P, T], F32, align_bytes=64, tag=tag, name="window")
-            nc.gpsimd.memset(window[:], 0.0)
+            engine.memset(window[:].bitcast(U32), 0)
             windows.append(window)
 
-        add_window("bytes0")
+        add_window(nc.vector, "bytes0")
 
         w0 = operand(P, "w0")
         interleave(by_scalar, w0, raw_w0, 0, 0, P)
@@ -115,7 +115,7 @@ def tile_list_hscat_none_kernel(tc, x, w, wgo, offs, out):
         w1 = operand(P, "w1", tag="bytes1")
         w2 = operand(2 * P, "w2", tag="bytes2")
         w4 = operand(4 * P, "w4")
-        x_second = [operand(BANK, "x4"), operand(BANK, "x5")]
+        x_second = [operand(BANK, "x4", tag="bytes3"), operand(BANK, "x5")]
         interleave(by_scalar, w1, raw_w1, 0, 0, P)
 
         weights_of = [(w0, 0), (w1, 0), (w2, 0), (w2, P)] + [(w4, m * P) for m in range(4)]
@@ -141,15 +141,14 @@ def tile_list_hscat_none_kernel(tc, x, w, wgo, offs, out):
 
         y = project(*steps[0])
         quantise(w1)
-        add_window("bytes1")
+        add_window(nc.gpsimd, "bytes1")
         y_next = project(*steps[1])
         scatter(*steps[0], y)
 
         interleave(by_scalar, w2, raw_w2, 0, 0, 2 * P)
         quantise(w2)
-        add_window("bytes2")
+        add_window(nc.gpsimd, "bytes2")
         interleave(by_scalar, x_second[0], raw_xd, 0, 0, BANK)
-        add_window("bytes3")
         interleave(by_scalar, x_second[1], raw_xe, 0, 0, BANK)
         y, y_next = y_next, project(*steps[2])
         scatter(*steps[1], y)
@@ -158,6 +157,7 @@ def tile_list_hscat_none_kernel(tc, x, w, wgo, offs, out):
         scatter(*steps[2], y)
 
         quantise(x_second[0])
+        add_window(nc.gpsimd, "bytes3")
         quantise(x_second[1])
         interleave(by_scalar, w4, raw_w4, 0, 0, 4 * P)
         quantise(w4)

from contextlib import ExitStack

import concourse.mybir as mybir

K, M, T, S = 512, 1024, 4096, 2048
FLOPS = 2 * K * M * S

F32 = mybir.dt.float32
BF16 = mybir.dt.bfloat16
U32 = mybir.dt.uint32
U16 = mybir.dt.uint16
U8 = mybir.dt.uint8
FP8X4 = mybir.dt.float8_e4m3fn_x4
MULT = mybir.AluOpType.mult

P = 128
PACK = 4
HALF = S // 2
HALF_OFFSETS = HALF // 16
PIECE = 256
BANK = 512
WINDOWS = 4
Y_BUFS = 6
VECTOR_SHARE = 160


def tile_list_hscat_none_kernel(tc, x, w, wgo, offs, out):
    nc = tc.nc
    with ExitStack() as ctx:
        lists = ctx.enter_context(tc.tile_pool(name="lists", bufs=1))
        keep = ctx.enter_context(tc.tile_pool(name="keep", bufs=1))
        products = ctx.enter_context(tc.tile_pool(name="products", bufs=Y_BUFS))
        psum = ctx.enter_context(tc.psum_pool(name="psum", bufs=8))

        def load(src, first, width, name):
            raw = keep.tile([P, PACK, width], F32, name="raw_" + name)
            nc.sync.dma_start(
                out=raw[:], in_=src[:, first : first + width].rearrange("(p i) c -> p i c", i=PACK)
            )
            return raw

        def operand(width, name, tag=None):
            grouped = keep.tile(
                [P, width, PACK], BF16, align_bytes=64, tag=tag or "grouped_" + name, name="grouped_" + name
            )
            codes = keep.tile([P, width], U32, align_bytes=64, name="codes_" + name)
            scales = keep.tile([P, width], U8, align_bytes=64, name="scales_" + name)
            return grouped, codes, scales

        def interleave(copy, op, raw, to, first, width):
            copy(
                out=op[0][:, to : to + width, :].rearrange("p (c b) i -> p c i b", b=4),
                in_=raw[:, :, first : first + width].rearrange("p i (c b) -> p c i b", b=4),
            )

        def quantise(op):
            grouped, codes, scales = op
            nc.vector.quantize_mx(
                out=codes[:].bitcast(FP8X4), scales=scales[:], in_=grouped[:].rearrange("p c i -> p (c i)")
            )

        def multiply(weights, first, x_op, width):
            acc = psum.tile([P, BANK], F32, name="acc")
            nc.tensor.matmul_mx(
                out=acc[:, :width],
                lhsT=weights[1][:, first : first + P].bitcast(FP8X4),
                lhsT_scale=weights[2][:, first : first + P],
                rhs=x_op[1][:].bitcast(FP8X4),
                rhs_scale=x_op[2][:],
                start=True,
                stop=True,
            )
            return acc

        by_vector, by_scalar = nc.vector.tensor_copy, nc.scalar.copy

        raw_w0 = load(w, 0, P, "w0")
        raw_xa = load(x, 0, 2 * PIECE, "xa")
        raw_xb = load(x, 2 * PIECE, PIECE, "xb")
        raw_xc = load(x, 3 * PIECE, PIECE, "xc")
        raw_w1 = load(w, P, P, "w1")
        offsets = lists.tile([P, S // 16], U16, name="offsets")
        nc.sync.dma_start(offsets[:], offs)
        wgo_halves = [keep.tile([P, HALF], F32, name="wgo0"), keep.tile([P, HALF], F32, name="wgo1")]
        nc.sync.dma_start(out=wgo_halves[0][:], in_=wgo[:, :HALF])
        raw_w2 = load(w, 2 * P, 2 * P, "w2")
        raw_xd = load(x, HALF, BANK, "xd")
        raw_xe = load(x, HALF + BANK, BANK, "xe")
        raw_w4 = load(w, 4 * P, 4 * P, "w4")
        nc.sync.dma_start(out=wgo_halves[1][:], in_=wgo[:, HALF:])

        windows = []

        def add_window(engine, tag):
            window = keep.tile([P, T], F32, align_bytes=64, tag=tag, name="window")
            engine.memset(window[:].bitcast(U32), 0)
            windows.append(window)

        add_window(nc.vector, "bytes0")

        w0 = operand(P, "w0")
        interleave(by_scalar, w0, raw_w0, 0, 0, P)
        quantise(w0)
        x_first = [operand(PIECE, "x0"), operand(PIECE, "x1"), operand(PIECE, "x2"), operand(PIECE, "x3")]
        interleave(by_scalar, x_first[0], raw_xa, 0, 0, PIECE)
        interleave(by_vector, x_first[1], raw_xa, 0, PIECE, PIECE)
        quantise(x_first[0])
        quantise(x_first[1])
        interleave(by_vector, x_first[2], raw_xb, 0, 0, PIECE)
        quantise(x_first[2])
        interleave(by_scalar, x_first[3], raw_xc, VECTOR_SHARE, VECTOR_SHARE, PIECE - VECTOR_SHARE)
        interleave(by_vector, x_first[3], raw_xc, 0, 0, VECTOR_SHARE)
        quantise(x_first[3])

        w1 = operand(P, "w1", tag="bytes1")
        w2 = operand(2 * P, "w2", tag="bytes2")
        w4 = operand(4 * P, "w4")
        x_second = [operand(BANK, "x4", tag="bytes3"), operand(BANK, "x5")]
        interleave(by_scalar, w1, raw_w1, 0, 0, P)

        weights_of = [(w0, 0), (w1, 0), (w2, 0), (w2, P)] + [(w4, m * P) for m in range(4)]

        def project(m, h):
            y = products.tile([P, HALF], F32, name="y")
            weights, first = weights_of[m]
            pieces, width = (x_first, PIECE) if h == 0 else (x_second, BANK)
            for q, piece in enumerate(pieces):
                acc = multiply(weights, first, piece, width)
                copy = by_vector if (m, h) == (0, 0) and q % 2 == 0 else by_scalar
                copy(out=y[:, q * width : (q + 1) * width], in_=acc[:, :width])
            return y

        steps = [(m, h) for group in (0, WINDOWS) for h in range(2) for m in range(group, group + WINDOWS)]

        def scatter(m, h, y):
            window = windows[m % WINDOWS]
            places = offsets[:, h * HALF_OFFSETS : (h + 1) * HALF_OFFSETS]
            nc.vector.tensor_tensor(window[:].indirect(places), y[:], wgo_halves[h][:], MULT)
            if h == 1:
                nc.sync.dma_start(out=out[m * P : (m + 1) * P, :], in_=window[:])

        y = project(*steps[0])
        quantise(w1)
        add_window(nc.gpsimd, "bytes1")
        y_next = project(*steps[1])
        scatter(*steps[0], y)

        interleave(by_scalar, w2, raw_w2, 0, 0, 2 * P)
        quantise(w2)
        add_window(nc.gpsimd, "bytes2")
        interleave(by_scalar, x_second[0], raw_xd, 0, 0, BANK)
        interleave(by_scalar, x_second[1], raw_xe, 0, 0, BANK)
        y, y_next = y_next, project(*steps[2])
        scatter(*steps[1], y)

        y, y_next = y_next, project(*steps[3])
        scatter(*steps[2], y)

        quantise(x_second[0])
        add_window(nc.gpsimd, "bytes3")
        quantise(x_second[1])
        interleave(by_scalar, w4, raw_w4, 0, 0, 4 * P)
        quantise(w4)
        for i in range(3, len(steps)):
            y = y_next
            if i + 1 < len(steps):
                y_next = project(*steps[i + 1])
            scatter(*steps[i], y)
